import numpy as np
import ml_dtypes

BF16 = ml_dtypes.bfloat16


def bf(x):
    return np.asarray(x, np.float32).astype(BF16)


def f32(x):
    return np.asarray(x, np.float32)


def f64(x):
    return np.asarray(x).astype(np.float64)


def striped(idx):
    return np.tile(idx.reshape(-1, 16).T, (8, 1))


def rows(idx, k):
    return np.tile(idx, (k, 1))


def look(tab, idx):
    return np.take_along_axis(f64(tab), rows(idx, len(tab)), axis=1)


K, S, V, N, M = 512, 2048, 1536, 1536, 512


def setup_inputs():
    return {"tab": f32(np.random.standard_normal((K, S))), "pos": f32(np.random.standard_normal((K, V))), "w": bf(np.random.standard_normal((K, M)) / np.sqrt(K)), "offs": striped(np.random.permutation(S)[:N])}


def reference(tab, pos, w, offs):
    idx = offs[:16].T.reshape(-1)
    x = np.maximum(look(tab, idx) - f64(pos) + 0.5, 0.0)
    y = f64(w).T @ x
    return y

@@ -1,0 +1,87 @@
+import concourse.mybir as mybir
+
+F32, BF16, U16 = mybir.dt.float32, mybir.dt.bfloat16, mybir.dt.uint16
+RELU = mybir.ActivationFunctionType.Relu
+
+P = 128
+K, S, N, M = 512, 2048, 1536, 512
+R = K // P
+MB = M // P
+J = 512
+NJ = N // J
+ENTRIES = 16
+MARGIN = 0.5
+
+FLOPS = 2 * K * M * N + 3 * K * N
+
+
+def tile_lookup_hinge_sub_none_kernel(tc, tab, pos, w, offs, out):
+    nc = tc.nc
+    with (
+        tc.tile_pool(name="held", bufs=1) as held,
+        tc.tile_pool(name="differences", bufs=3) as differences,
+        tc.tile_pool(name="results", bufs=4) as results,
+        tc.psum_pool(name="sums", bufs=8) as sums,
+    ):
+        offsets = held.tile([P, N // ENTRIES], U16, name="offsets")
+        nc.sync.dma_start(offsets[:], offs)
+
+        tables, positives = [], []
+        weights = held.tile([P, R, M], BF16, name="weights")
+        for r in range(R):
+            table = held.tile([P, S], F32, name=f"table_{r}")
+            nc.sync.dma_start(table[:], tab[r * P : (r + 1) * P, :])
+            positive = held.tile([P, N], F32, name=f"positive_{r}")
+            nc.sync.dma_start(positive[:], pos[r * P : (r + 1) * P, :])
+            tables.append(table)
+            positives.append(positive)
+            if r == 0:
+                nc.sync.dma_start(weights[:], w.rearrange("(k p) m -> p k m", p=P))
+
+        margin = held.tile([P, 1], F32, name="margin")
+        nc.vector.memset(margin[:], MARGIN)
+
+        x = [[held.tile([P, J], BF16, name=f"x_{r}_{j}") for j in range(NJ)] for r in range(R)]
+
+        def look_up(r, j):
+            difference = differences.tile([P, J], F32, name="difference")
+            piece = offsets[:, j * (J // ENTRIES) : (j + 1) * (J // ENTRIES)]
+            nc.vector.tensor_tensor(
+                difference[:],
+                tables[r][:].indirect(piece),
+                positives[r][:, j * J : (j + 1) * J],
+                mybir.AluOpType.subtract,
+            )
+            nc.scalar.activation(x[r][j][:], difference[:], RELU, bias=margin[:])
+
+        def multiply(bank, r, j, m):
+            nc.tensor.matmul(
+                bank[:], weights[:, r, m * P : (m + 1) * P], x[r][j][:], start=(r == 0), stop=(r == R - 1)
+            )
+
+        def store(bank, j, m):
+            result = results.tile([P, J], F32, name="result")
+            if m % 2 == 0:
+                nc.scalar.copy(result[:], bank[:])
+            else:
+                nc.vector.tensor_copy(result[:], bank[:])
+            nc.sync.dma_start(out[m * P : (m + 1) * P, j * J : (j + 1) * J], result[:])
+
+        early = range(NJ - 1)
+        banks = {(j, m): sums.tile([P, J], F32, name=f"sum_{j}_{m}", tag="sum") for j in early for m in range(MB)}
+        for r in range(R):
+            for j in range(NJ):
+                look_up(r, j)
+            for j in early:
+                for m in range(MB):
+                    multiply(banks[j, m], r, j, m)
+        for j in early:
+            for m in range(MB):
+                store(banks[j, m], j, m)
+
+        last = NJ - 1
+        for m in range(MB):
+            bank = sums.tile([P, J], F32, name=f"sum_{last}_{m}", tag="sum")
+            for r in range(R):
+                multiply(bank, r, last, m)
+            store(bank, last, m)

@@ -11,6 +11,7 @@ J = 512
 NJ = N // J
 ENTRIES = 16
 MARGIN = 0.5
+ALL, FIRST_HALF, SECOND_HALF = range(R), range(R // 2), range(R // 2, R)
 
 FLOPS = 2 * K * M * N + 3 * K * N
 
@@ -20,23 +21,29 @@ def tile_lookup_hinge_sub_none_kernel(tc, tab, pos, w, offs, out):
     with (
         tc.tile_pool(name="held", bufs=1) as held,
         tc.tile_pool(name="differences", bufs=3) as differences,
-        tc.tile_pool(name="results", bufs=4) as results,
+        tc.tile_pool(name="results", bufs=NJ * MB) as results,
         tc.psum_pool(name="sums", bufs=8) as sums,
     ):
         offsets = held.tile([P, N // ENTRIES], U16, name="offsets")
         nc.sync.dma_start(offsets[:], offs)
 
-        tables, positives = [], []
+        tables = [held.tile([P, S], F32, name=f"table_{r}") for r in range(R)]
+        positives = [held.tile([P, N], F32, name=f"positive_{r}") for r in range(R)]
         weights = held.tile([P, R, M], BF16, name="weights")
+
+        def load_rest(r):
+            nc.sync.dma_start(positives[r][:, J:], pos[r * P : (r + 1) * P, J:])
+
         for r in range(R):
-            table = held.tile([P, S], F32, name=f"table_{r}")
-            nc.sync.dma_start(table[:], tab[r * P : (r + 1) * P, :])
-            positive = held.tile([P, N], F32, name=f"positive_{r}")
-            nc.sync.dma_start(positive[:], pos[r * P : (r + 1) * P, :])
-            tables.append(table)
-            positives.append(positive)
+            rows = slice(r * P, (r + 1) * P)
+            nc.sync.dma_start(tables[r][:], tab[rows, :])
+            nc.sync.dma_start(positives[r][:, :J], pos[rows, :J])
+            if r in FIRST_HALF:
+                load_rest(r)
             if r == 0:
                 nc.sync.dma_start(weights[:], w.rearrange("(k p) m -> p k m", p=P))
+        for r in SECOND_HALF:
+            load_rest(r)
 
         margin = held.tile([P, 1], F32, name="margin")
         nc.vector.memset(margin[:], MARGIN)
@@ -54,34 +61,53 @@ def tile_lookup_hinge_sub_none_kernel(tc, tab, pos, w, offs, out):
             )
             nc.scalar.activation(x[r][j][:], difference[:], RELU, bias=margin[:])
 
-        def multiply(bank, r, j, m):
-            nc.tensor.matmul(
-                bank[:], weights[:, r, m * P : (m + 1) * P], x[r][j][:], start=(r == 0), stop=(r == R - 1)
-            )
+        def open_banks(name):
+            return [sums.tile([P, J], F32, name=f"{name}_{m}", tag="sum") for m in range(MB)]
 
-        def store(bank, j, m):
+        def multiply(banks, r, j, rows):
+            for m in range(MB):
+                nc.tensor.matmul(
+                    banks[m][:],
+                    weights[:, r, m * P : (m + 1) * P],
+                    x[r][j][:],
+                    start=(r == rows[0]),
+                    stop=(r == rows[-1]),
+                )
+
+        def store(j, m, take):
             result = results.tile([P, J], F32, name="result")
-            if m % 2 == 0:
-                nc.scalar.copy(result[:], bank[:])
-            else:
-                nc.vector.tensor_copy(result[:], bank[:])
+            take(result)
             nc.sync.dma_start(out[m * P : (m + 1) * P, j * J : (j + 1) * J], result[:])
 
-        early = range(NJ - 1)
-        banks = {(j, m): sums.tile([P, J], F32, name=f"sum_{j}_{m}", tag="sum") for j in early for m in range(MB)}
-        for r in range(R):
+        piece_0 = open_banks("piece_0")
+        piece_2_first = open_banks("piece_2_first")
+        for r in FIRST_HALF:
             for j in range(NJ):
                 look_up(r, j)
-            for j in early:
-                for m in range(MB):
-                    multiply(banks[j, m], r, j, m)
-        for j in early:
-            for m in range(MB):
-                store(banks[j, m], j, m)
-
-        last = NJ - 1
+            multiply(piece_0, r, 0, ALL)
+            multiply(piece_2_first, r, 2, FIRST_HALF)
+        carried = [held.tile([P, J], F32, name=f"carried_{m}") for m in range(MB)]
         for m in range(MB):
-            bank = sums.tile([P, J], F32, name=f"sum_{last}_{m}", tag="sum")
-            for r in range(R):
-                multiply(bank, r, last, m)
-            store(bank, last, m)
+            nc.scalar.copy(carried[m][:], piece_2_first[m][:])
+
+        piece_1 = open_banks("piece_1")
+        for r in FIRST_HALF:
+            multiply(piece_1, r, 1, ALL)
+
+        for r in SECOND_HALF:
+            look_up(r, 0)
+            multiply(piece_0, r, 0, ALL)
+        for m in range(MB):
+            store(0, m, lambda result: nc.scalar.copy(result[:], piece_0[m][:]))
+        piece_2 = open_banks("piece_2")
+        for r in SECOND_HALF:
+            look_up(r, 1)
+            multiply(piece_1, r, 1, ALL)
+        for r in SECOND_HALF:
+            look_up(r, 2)
+            multiply(piece_2, r, 2, SECOND_HALF)
+        for m in range(MB):
+            copy = nc.scalar.copy if m % 2 == 0 else nc.vector.tensor_copy
+            store(1, m, lambda result: copy(result[:], piece_1[m][:]))
+        for m in range(MB):
+            store(2, m, lambda result: nc.vector.tensor_add(result[:], piece_2[m][:], carried[m][:]))

import concourse.mybir as mybir

F32, BF16, U16 = mybir.dt.float32, mybir.dt.bfloat16, mybir.dt.uint16
RELU = mybir.ActivationFunctionType.Relu

P = 128
K, S, N, M = 512, 2048, 1536, 512
R = K // P
MB = M // P
J = 512
NJ = N // J
ENTRIES = 16
MARGIN = 0.5
ALL, FIRST_HALF, SECOND_HALF = range(R), range(R // 2), range(R // 2, R)

FLOPS = 2 * K * M * N + 3 * K * N


def tile_lookup_hinge_sub_none_kernel(tc, tab, pos, w, offs, out):
    nc = tc.nc
    with (
        tc.tile_pool(name="held", bufs=1) as held,
        tc.tile_pool(name="differences", bufs=3) as differences,
        tc.tile_pool(name="results", bufs=NJ * MB) as results,
        tc.psum_pool(name="sums", bufs=8) as sums,
    ):
        offsets = held.tile([P, N // ENTRIES], U16, name="offsets")
        nc.sync.dma_start(offsets[:], offs)

        tables = [held.tile([P, S], F32, name=f"table_{r}") for r in range(R)]
        positives = [held.tile([P, N], F32, name=f"positive_{r}") for r in range(R)]
        weights = held.tile([P, R, M], BF16, name="weights")

        def load_rest(r):
            nc.sync.dma_start(positives[r][:, J:], pos[r * P : (r + 1) * P, J:])

        for r in range(R):
            rows = slice(r * P, (r + 1) * P)
            nc.sync.dma_start(tables[r][:], tab[rows, :])
            nc.sync.dma_start(positives[r][:, :J], pos[rows, :J])
            if r in FIRST_HALF:
                load_rest(r)
            if r == 0:
                nc.sync.dma_start(weights[:], w.rearrange("(k p) m -> p k m", p=P))
        for r in SECOND_HALF:
            load_rest(r)

        margin = held.tile([P, 1], F32, name="margin")
        nc.vector.memset(margin[:], MARGIN)

        x = [[held.tile([P, J], BF16, name=f"x_{r}_{j}") for j in range(NJ)] for r in range(R)]

        def look_up(r, j):
            difference = differences.tile([P, J], F32, name="difference")
            piece = offsets[:, j * (J // ENTRIES) : (j + 1) * (J // ENTRIES)]
            nc.vector.tensor_tensor(
                difference[:],
                tables[r][:].indirect(piece),
                positives[r][:, j * J : (j + 1) * J],
                mybir.AluOpType.subtract,
            )
            nc.scalar.activation(x[r][j][:], difference[:], RELU, bias=margin[:])

        def open_banks(name):
            return [sums.tile([P, J], F32, name=f"{name}_{m}", tag="sum") for m in range(MB)]

        def multiply(banks, r, j, rows):
            for m in range(MB):
                nc.tensor.matmul(
                    banks[m][:],
                    weights[:, r, m * P : (m + 1) * P],
                    x[r][j][:],
                    start=(r == rows[0]),
                    stop=(r == rows[-1]),
                )

        def store(j, m, take):
            result = results.tile([P, J], F32, name="result")
            take(result)
            nc.sync.dma_start(out[m * P : (m + 1) * P, j * J : (j + 1) * J], result[:])

        piece_0 = open_banks("piece_0")
        piece_2_first = open_banks("piece_2_first")
        for r in FIRST_HALF:
            for j in range(NJ):
                look_up(r, j)
            multiply(piece_0, r, 0, ALL)
            multiply(piece_2_first, r, 2, FIRST_HALF)
        carried = [held.tile([P, J], F32, name=f"carried_{m}") for m in range(MB)]
        for m in range(MB):
            nc.scalar.copy(carried[m][:], piece_2_first[m][:])

        piece_1 = open_banks("piece_1")
        for r in FIRST_HALF:
            multiply(piece_1, r, 1, ALL)

        for r in SECOND_HALF:
            look_up(r, 0)
            multiply(piece_0, r, 0, ALL)
        for m in range(MB):
            store(0, m, lambda result: nc.scalar.copy(result[:], piece_0[m][:]))
        piece_2 = open_banks("piece_2")
        for r in SECOND_HALF:
            look_up(r, 1)
            multiply(piece_1, r, 1, ALL)
        for r in SECOND_HALF:
            look_up(r, 2)
            multiply(piece_2, r, 2, SECOND_HALF)
        for m in range(MB):
            copy = nc.scalar.copy if m % 2 == 0 else nc.vector.tensor_copy
            store(1, m, lambda result: copy(result[:], piece_1[m][:]))
        for m in range(MB):
            store(2, m, lambda result: nc.vector.tensor_add(result[:], piece_2[m][:], carried[m][:]))
